import numpy as np
import ml_dtypes


def mxq(x, axis, fmt="e4m3"):
    dtype, down = {"e4m3": (ml_dtypes.float8_e4m3fn, 7), "e5m2": (ml_dtypes.float8_e5m2, 14)}[fmt]
    v = np.moveaxis(np.asarray(x, np.float32).astype(ml_dtypes.bfloat16).astype(np.float64), axis, -1)
    blocks = v.reshape(v.shape[:-1] + (-1, 32))
    amax = np.abs(blocks).max(-1, keepdims=True)
    byte = np.maximum(np.where(amax > 0, np.frexp(amax)[1] - 1 + 127, 0) - down, 1)
    scale = np.exp2(byte - 127.0)
    codes = (blocks / scale).astype(np.float32).astype(dtype).astype(np.float64)
    return np.moveaxis((codes * scale).reshape(v.shape), -1, axis)


WIDE = False


def mx_kscale(k):
    if not WIDE:
        return np.ones(k)
    levels = np.array([10, -10, 5, -5, 0])
    if k % 512:
        return np.exp2(np.random.permutation(np.resize(levels, k // 32))).repeat(32)
    a = np.empty((k // 512, 16))
    for p in range(k // 512):
        a[p, :8] = np.random.permutation(np.resize(levels, 8))
        for g in range(8):
            far = levels[np.abs(levels - a[p, g]) >= 10]
            a[p, g + 8] = far[np.random.randint(len(far))]
    return np.exp2(a.ravel()).repeat(32)


def f64(x):
    return np.asarray(x).astype(np.float64)


def striped(idx):
    return np.tile(idx.reshape(-1, 16).T, (8, 1)).astype(np.uint16)


def unstriped(offs):
    return offs[:16].T.reshape(-1).astype(np.int64)


E2M1 = np.array([0.0, 0.5, 1.0, 1.5, 2.0, 3.0, 4.0, 6.0, -0.0, -0.5, -1.0, -1.5, -2.0, -3.0, -4.0, -6.0])


def pack_weight(w, fmt):
    k, n = w.shape
    w = f64(np.asarray(w, np.float32).astype(ml_dtypes.bfloat16)).reshape(k // 32, 32, n)
    amax = np.abs(w).max(1)
    if fmt == "e4m3":
        byte = np.frexp(amax)[1] - 1 + 127 - 7
    else:
        mant, ex = np.frexp(amax / 6.0)
        byte = np.where(mant > 0.5, ex, ex - 1) + 127
    byte = np.clip(np.where(amax > 0, byte, 1), 1, 254)
    scaled = (w * np.exp2(127.0 - byte)[:, None, :]).reshape(k, n).astype(np.float32)
    by_word = np.ascontiguousarray(scaled.reshape(k // 512, 128, 4, n).transpose(0, 1, 3, 2))
    if fmt == "e4m3":
        words = by_word.astype(ml_dtypes.float8_e4m3fn).view(np.uint8)
    else:
        c = by_word.astype(ml_dtypes.float4_e2m1fn).view(np.uint8) & 0xF
        words = (c[..., 0::2] | (c[..., 1::2] << 4)).reshape(k // 512, 128, 2 * n)
    return np.ascontiguousarray(words), np.ascontiguousarray(byte.astype(np.uint8).reshape(k // 512, 16, n))


def unpack_weight(words, scales, fmt):
    g, _, n = scales.shape
    words = np.ascontiguousarray(words).reshape(g, 128, n, -1)
    if fmt == "e4m3":
        vals = words.view(ml_dtypes.float8_e4m3fn).astype(np.float64)
    else:
        nib = np.empty((g, 128, n, 4), np.uint8)
        nib[..., 0::2] = words & 0xF
        nib[..., 1::2] = words >> 4
        vals = E2M1[nib]
    vals = vals * np.repeat(np.exp2(scales.astype(np.float64) - 127.0), 8, axis=1)[..., None]
    return vals.transpose(0, 1, 3, 2).reshape(g * 512, n)


def gelu(v):
    return 0.5 * v * (1.0 + np.tanh(np.sqrt(2.0 / np.pi) * (v + 0.044715 * v**3)))


def bf(x):
    return np.asarray(x, np.float32).astype(ml_dtypes.bfloat16)


def planes(Y):
    n, m = Y.shape
    b = f64(bf(Y)).reshape(n // 32, 32, m)
    amax = np.abs(b).max(1)
    byte = np.clip(np.where(amax > 0, np.frexp(amax)[1] - 1 + 127 - 7, 1), 1, 254)
    codes = (b * np.exp2(127.0 - byte)[:, None, :]).reshape(n, m).astype(np.float32).astype(ml_dtypes.float8_e4m3fn).view(np.uint8)
    words = codes.reshape(n // 512, 128, 4, m).transpose(0, 1, 3, 2)
    return np.ascontiguousarray(words), np.ascontiguousarray(byte.astype(np.uint8).reshape(n // 512, 16, m))


K, H, N, T, S, P = 1024, 1024, 512, 2048, 1024, 512

def setup_inputs():
    n = np.random.standard_normal
    s = mx_kscale(K)[:, None]
    u = mx_kscale(H)[:, None]
    tab_words, tab_scales = pack_weight(n((K, T)) * s, "e4m3")
    w1 = n((K, H)) / np.sqrt(K) / s * u.T
    w2_words, w2_scales = pack_weight(n((K, H)) / np.sqrt(K) / s * u.T, "e2m1")
    w3_words, w3_scales = pack_weight(0.66 * n((H, N)) / np.sqrt(H) / u, "e4m3")
    res = 0.5 * n((H, S)) * u
    temp = np.random.uniform(0.4, 1.6, N)
    sway = np.random.choice([-1.0, 1.0], N) * np.random.uniform(3.0, 7.0, N)
    base = 0.7 * n((N, P))
    gain = np.exp(0.8 * n(N))
    return {
        "tab_words": tab_words, "tab_scales": tab_scales,
        "offs": striped(np.random.permutation(T)[:S]),
        "pos1": striped(np.random.permutation(S)[:P]),
        "pos2": striped(np.random.permutation(S)[:P]),
        "w1": w1.astype(np.float32),
        "w2_words": w2_words, "w2_scales": w2_scales,
        "w3_words": w3_words, "w3_scales": w3_scales,
        "res": res.astype(np.float32),
        "temp": temp.astype(np.float32),
        "sway": sway.astype(np.float32),
        "base": base.astype(np.float32),
        "gain": gain.astype(np.float32),
    }

def reference(tab_words, tab_scales, offs, pos1, pos2, w1, w2_words, w2_scales, w3_words, w3_scales, res, temp, sway, base, gain):
    v = unpack_weight(tab_words, tab_scales, "e4m3")[:, unstriped(offs)]
    w1q = mxq(f64(w1), 0, "e4m3")
    w2 = unpack_weight(w2_words, w2_scales, "e2m1")
    w3 = unpack_weight(w3_words, w3_scales, "e4m3")
    h = np.maximum(w1q.T @ v, w2.T @ v) + f64(res)
    hq = mxq(h, 0, "e4m3")
    e = w3.T @ hq
    top = e.max(axis=1)
    a = np.exp(f64(temp)[:, None] * (e[:, unstriped(pos1)] - top[:, None]))
    c = np.maximum(e[:, unstriped(pos2)], f64(base))
    y = f64(gain)[:, None] * (f64(sway)[:, None] * a + c)
    words, scales = planes(y)
    return y, words, scales

@@ -1,0 +1,266 @@
+from contextlib import ExitStack
+
+import concourse.mybir as mybir
+
+K, H, N, T, S, PICK = 1024, 1024, 512, 2048, 1024, 512
+FLOPS = 2 * (2 * K * H * S + H * N * S)
+
+F32 = mybir.dt.float32
+BF16 = mybir.dt.bfloat16
+I32 = mybir.dt.int32
+U32 = mybir.dt.uint32
+U16 = mybir.dt.uint16
+U8 = mybir.dt.uint8
+FP8X4 = mybir.dt.float8_e4m3fn_x4
+FP4X4 = mybir.dt.float4_e2m1fn_x4
+ALU = mybir.AluOpType
+ACT = mybir.ActivationFunctionType
+
+P = 128
+PACK = 4
+PASS = P * PACK
+HALF = 512
+QUADS = 4
+
+
+def tile_list_monsoon_onset_outlook_kernel(
+    tc, tab_words, tab_scales, offs, pos1, pos2, w1, w2_words, w2_scales, w3_words, w3_scales,
+    res, temp, sway, base, gain, out_0, out_1, out_2,
+):
+    nc = tc.nc
+    with ExitStack() as ctx:
+        lists = ctx.enter_context(tc.tile_pool(name="lists", bufs=1))
+        keep = ctx.enter_context(tc.tile_pool(name="keep", bufs=1))
+        ring = ctx.enter_context(tc.tile_pool(name="ring", bufs=2))
+        psum = ctx.enter_context(tc.psum_pool(name="psum", bufs=4))
+
+        def kept(shape, dtype, name):
+            return keep.tile(shape, dtype, name=name, align_bytes=64)
+
+        offs_sb = lists.tile([P, S // 16], U16, name="offs_sb")
+        pos1_sb = lists.tile([P, PICK // 16], U16, name="pos1_sb")
+        pos2_sb = lists.tile([P, PICK // 16], U16, name="pos2_sb")
+
+        tab_s = kept([P, 2 * T], U8, "tab_s")
+        w2_s = kept([P, 2 * H], U8, "w2_s")
+        w3_s = kept([P, N], U8, "w3_s")
+        nc.gpsimd.memset(tab_s[:].bitcast(I32), 0)
+        nc.vector.memset(w2_s[:].bitcast(I32), 0)
+        nc.vector.memset(w3_s[:].bitcast(I32), 0)
+
+        def load_scale_rows(plane, rows):
+            for q in range(QUADS):
+                nc.gpsimd.dma_start(
+                    out=plane[32 * q : 32 * q + 4, :].bitcast(I32).rearrange("r (a c) -> r a c", a=2),
+                    in_=rows[:, 4 * q : 4 * q + 4, :].bitcast(I32).rearrange("a r c -> r a c"),
+                )
+
+        tab_w = [kept([P, T], I32, f"tab_w{a}") for a in range(2)]
+        w2_w = kept([P, 2, H // 2], I32, "w2_w")
+        w3_w = kept([P, 2, N], I32, "w3_w")
+        w1_raw = {(a, b): kept([P, PACK, PASS], F32, f"w1_raw{a}{b}") for a in range(2) for b in range(2)}
+        res_sb = {(b, h): kept([P, PACK, HALF], F32, f"res{b}{h}") for b in range(2) for h in range(2)}
+        base_sb = kept([P, PACK, PICK], F32, "base_sb")
+        temp_sb = kept([P, PACK], F32, "temp_sb")
+        sway_sb = kept([P, PACK], F32, "sway_sb")
+        gain_sb = kept([P, PACK], F32, "gain_sb")
+
+        def load_w1(a, b):
+            rows = w1[PASS * a : PASS * (a + 1), PASS * b : PASS * (b + 1)]
+            nc.sync.dma_start(out=w1_raw[a, b][:], in_=rows.rearrange("(p i) c -> p i c", i=PACK))
+
+        def load_res(b, h):
+            rows = res[PASS * b : PASS * (b + 1), HALF * h : HALF * (h + 1)]
+            nc.sync.dma_start(out=res_sb[b, h][:], in_=rows.rearrange("(p t) j -> p t j", t=PACK))
+
+        nc.sync.dma_start(offs_sb[:], offs)
+        load_scale_rows(tab_s, tab_scales)
+        for a in range(2):
+            nc.sync.dma_start(out=tab_w[a][:], in_=tab_words[a].rearrange("p t i -> p (t i)").bitcast(I32))
+        nc.sync.dma_start(out=w2_w[:], in_=w2_words.bitcast(I32).rearrange("a p c -> p a c"))
+        load_scale_rows(w2_s, w2_scales)
+        load_w1(0, 0)
+        load_w1(1, 0)
+        load_res(0, 0)
+        load_w1(0, 1)
+        load_w1(1, 1)
+        load_res(0, 1)
+        for q in range(QUADS):
+            nc.sync.dma_start(
+                out=w3_s[32 * q : 32 * q + 8, :].bitcast(I32),
+                in_=w3_scales[:, 4 * q : 4 * q + 4, :].bitcast(I32),
+            )
+        load_res(1, 0)
+        nc.sync.dma_start(
+            out=w3_w[:], in_=w3_words.rearrange("a p c i -> a p (c i)").bitcast(I32).rearrange("a p c -> p a c")
+        )
+        load_res(1, 1)
+        for vec_sb, vec in ((temp_sb, temp), (sway_sb, sway), (gain_sb, gain)):
+            nc.sync.dma_start(out=vec_sb[:], in_=vec.rearrange("(p t) -> p t", t=PACK))
+        nc.sync.dma_start(pos1_sb[:], pos1)
+        nc.sync.dma_start(pos2_sb[:], pos2)
+        nc.sync.dma_start(out=base_sb[:], in_=base.rearrange("(p t) m -> p t m", t=PACK))
+
+        v_w, v_s = {}, {}
+
+        def gather_table(h):
+            entries = offs_sb[:, (HALF // 16) * h : (HALF // 16) * (h + 1)]
+            for a in range(2):
+                v_w[a, h] = kept([P, HALF], U32, f"v_w{a}{h}")
+                nc.vector.tensor_copy(out=v_w[a, h][:], in_=tab_w[a][:].bitcast(U32).indirect(entries))
+            for a in range(2):
+                v_s[a, h] = kept([P, HALF], U8, f"v_s{a}{h}")
+                nc.vector.tensor_copy(out=v_s[a, h][:], in_=tab_s[:, T * a : T * (a + 1)].indirect(entries))
+
+        w2_wd = kept([P, 2, 2, PACK, P], U16, "w2_wd")
+        w2_sd = kept([P, 2, 2, PACK, P], U8, "w2_sd")
+
+        def deal_w2():
+            nc.vector.tensor_copy(
+                out=w2_sd[:].rearrange("p a b t m -> p (a b) t m"),
+                in_=w2_s[:].rearrange("p (ab m t) -> p ab t m", t=PACK, m=P),
+            )
+            for a in range(2):
+                nc.scalar.copy(
+                    out=w2_wd[:, a],
+                    in_=w2_w[:, a, :].bitcast(U16).rearrange("p (b m t) -> p b t m", t=PACK, m=P),
+                )
+
+        w1_w, w1_s = {}, {}
+
+        def quantize_w1(a, b):
+            grouped = ring.tile([P, PACK, P, PACK], BF16, name="w1_grouped", align_bytes=64)
+            nc.scalar.copy(
+                out=grouped[:].rearrange("p t m i -> p m i t"),
+                in_=w1_raw[a, b][:].rearrange("p i (m t) -> p m i t", t=PACK),
+            )
+            w1_w[a, b] = kept([P, PASS], U32, f"w1_w{a}{b}")
+            w1_s[a, b] = kept([P, PASS], U8, f"w1_s{a}{b}")
+            nc.vector.quantize_mx(
+                out=w1_w[a, b][:].bitcast(FP8X4), scales=w1_s[a, b][:],
+                in_=grouped[:].rearrange("p t m i -> p (t m i)"),
+            )
+
+        h_w, h_s = {}, {}
+
+        def first_stage(b, h, adder):
+            best = kept([P, PACK, HALF], F32, f"best{b}{h}")
+            for t in range(PACK):
+                acc = psum.tile([P, HALF], F32, name="acc1")
+                for a in range(2):
+                    nc.tensor.matmul_mx(
+                        out=acc[:], lhsT=w2_wd[:, a, b, t, :].bitcast(FP4X4), lhsT_scale=w2_sd[:, a, b, t, :],
+                        rhs=v_w[a, h][:].bitcast(FP8X4), rhs_scale=v_s[a, h][:], start=(a == 0), stop=(a == 1),
+                    )
+                nc.scalar.copy(out=best[:, t, :], in_=acc[:])
+            for t in range(PACK):
+                acc = psum.tile([P, HALF], F32, name="acc1")
+                cols = slice(P * t, P * (t + 1))
+                for a in range(2):
+                    nc.tensor.matmul_mx(
+                        out=acc[:], lhsT=w1_w[a, b][:, cols].bitcast(FP8X4), lhsT_scale=w1_s[a, b][:, cols],
+                        rhs=v_w[a, h][:].bitcast(FP8X4), rhs_scale=v_s[a, h][:], start=(a == 0), stop=(a == 1),
+                    )
+                nc.vector.tensor_tensor(out=best[:, t, :], in0=acc[:], in1=best[:, t, :], op=ALU.max)
+            grouped = ring.tile([P, HALF * PACK], BF16, name="h_grouped", align_bytes=64)
+            width = HALF // 1
+            for piece in range(1):
+                cols = slice(width * piece, width * (piece + 1))
+                adder.tensor_tensor(
+                    out=grouped[:, PACK * cols.start : PACK * cols.stop].rearrange("p (c i t) -> p c t i", i=2, t=PACK),
+                    in0=best[:, :, cols].rearrange("p t (c i) -> p c t i", i=2),
+                    in1=res_sb[b, h][:, :, cols].rearrange("p t (c i) -> p c t i", i=2),
+                    op=ALU.add,
+                )
+            h_w[b, h] = kept([P, HALF], U32, f"h_w{b}{h}")
+            h_s[b, h] = kept([P, HALF], U8, f"h_s{b}{h}")
+            nc.vector.quantize_mx(out=h_w[b, h][:].bitcast(FP8X4), scales=h_s[b, h][:], in_=grouped[:])
+
+        w3_wd = kept([P, 2, PACK, P], U32, "w3_wd")
+        w3_sd = kept([P, PACK, P], U8, "w3_sd")
+
+        def deal_w3():
+            nc.vector.tensor_copy(out=w3_sd[:], in_=w3_s[:].rearrange("p (m t) -> p t m", t=PACK))
+            nc.scalar.copy(
+                out=w3_wd[:].rearrange("p a t m -> p a m t"),
+                in_=w3_w[:].bitcast(U32).rearrange("p a (m t) -> p a m t", t=PACK),
+            )
+
+        e_sb = [kept([P, S], F32, f"e{t}") for t in range(PACK)]
+        top = [kept([P, PACK], F32, f"top{h}") for h in range(2)]
+
+        def second_stage(h, t):
+            acc = psum.tile([P, HALF], F32, name="acc2")
+            for b in range(2):
+                nc.tensor.matmul_mx(
+                    out=acc[:], lhsT=w3_wd[:, b, t, :].bitcast(FP8X4), lhsT_scale=w3_sd[4 * b : P, t, :],
+                    rhs=h_w[b, h][:].bitcast(FP8X4), rhs_scale=h_s[b, h][:], start=(b == 0), stop=(b == 1),
+                )
+            nc.vector.tensor_scalar(
+                out=e_sb[t][:, HALF * h : HALF * (h + 1)], in0=acc[:], scalar1=1.0,
+                scalar2=None if h == 0 else top[0][:, t : t + 1],
+                op0=ALU.mult, op1=ALU.max, accum_out=top[h][:, t : t + 1],
+            )
+
+        neg_temp = kept([P, PACK], F32, "neg_temp")
+        gain_sway = kept([P, PACK], F32, "gain_sway")
+        shift = kept([P, PACK], F32, "shift")
+        y = kept([P, PACK, PICK], F32, "y")
+
+        def row_constants():
+            nc.gpsimd.tensor_scalar(out=neg_temp[:], in0=temp_sb[:], scalar1=-1.0, scalar2=0.0, op0=ALU.mult, op1=ALU.add)
+            nc.gpsimd.tensor_tensor(out=gain_sway[:], in0=gain_sb[:], in1=sway_sb[:], op=ALU.mult)
+            for t in range(PACK):
+                nc.scalar.activation(out=base_sb[:, t, :], in_=base_sb[:, t, :], func=ACT.Copy, scale=gain_sb[:, t : t + 1])
+
+        def looks(t):
+            col = slice(t, t + 1)
+            nc.scalar.activation(out=shift[:, col], in_=top[1][:, col], func=ACT.Copy, scale=neg_temp[:, col])
+            onset = ring.tile([P, PICK], F32, name="onset")
+            nc.scalar.activation(
+                out=onset[:], in_=e_sb[t][:].indirect(pos1_sb[:]), func=ACT.Exp, bias=shift[:, col], scale=temp_sb[:, col]
+            )
+            dry = ring.tile([P, PICK], F32, name="dry")
+            nc.vector.tensor_copy(out=dry[:], in_=e_sb[t][:].indirect(pos2_sb[:]))
+            nc.vector.scalar_tensor_tensor(
+                out=dry[:], in0=dry[:], scalar=gain_sb[:, col], in1=base_sb[:, t, :], op0=ALU.mult, op1=ALU.max
+            )
+            nc.vector.scalar_tensor_tensor(
+                out=y[:, t, :], in0=onset[:], scalar=gain_sway[:, col], in1=dry[:], op0=ALU.mult, op1=ALU.add
+            )
+            nc.sync.dma_start(out=out_0.rearrange("(p t) m -> p t m", t=PACK)[:, t, :], in_=y[:, t, :])
+
+        gather_table(0)
+        deal_w2()
+        quantize_w1(0, 0)
+        quantize_w1(1, 0)
+        first_stage(0, 0, nc.vector)
+        gather_table(1)
+        quantize_w1(0, 1)
+        quantize_w1(1, 1)
+        first_stage(0, 1, nc.vector)
+        first_stage(1, 0, nc.vector)
+        deal_w3()
+        first_stage(1, 1, nc.vector)
+        for t in range(PACK):
+            second_stage(0, t)
+        row_constants()
+        for t in range(PACK):
+            second_stage(1, t)
+        for t in range(PACK):
+            looks(t)
+
+        y_grouped = kept([P, PICK * PACK], BF16, "y_grouped")
+        split = 320
+        for engine_copy, cols in ((nc.vector.tensor_copy, slice(0, split)), (nc.scalar.copy, slice(split, PICK))):
+            engine_copy(
+                out=y_grouped[:, PACK * cols.start : PACK * cols.stop].rearrange("p (c i t) -> p c t i", i=4, t=PACK),
+                in_=y[:, :, cols].rearrange("p t (c i) -> p c t i", i=4),
+            )
+        y_w = kept([P, PICK], U32, "y_w")
+        y_s = kept([P, PICK], U8, "y_s")
+        nc.vector.quantize_mx(out=y_w[:].bitcast(FP8X4), scales=y_s[:], in_=y_grouped[:])
+        nc.sync.dma_start(out=out_1[0].rearrange("p m t -> p (m t)").bitcast(I32), in_=y_w[:].bitcast(I32))
+        for q in range(QUADS):
+            queue = nc.scalar if q % 2 else nc.sync
+            queue.dma_start(out=out_2[0, 4 * q : 4 * q + 4, :].bitcast(I32), in_=y_s[32 * q : 32 * q + 4, :].bitcast(I32))

@@ -32,7 +32,8 @@ def tile_list_monsoon_onset_outlook_kernel(
         lists = ctx.enter_context(tc.tile_pool(name="lists", bufs=1))
         keep = ctx.enter_context(tc.tile_pool(name="keep", bufs=1))
         ring = ctx.enter_context(tc.tile_pool(name="ring", bufs=2))
-        psum = ctx.enter_context(tc.psum_pool(name="psum", bufs=4))
+        stage = ctx.enter_context(tc.tile_pool(name="stage", bufs=1))
+        psum = ctx.enter_context(tc.psum_pool(name="psum", bufs=1))
 
         def kept(shape, dtype, name):
             return keep.tile(shape, dtype, name=name, align_bytes=64)
@@ -44,21 +45,29 @@ def tile_list_monsoon_onset_outlook_kernel(
         tab_s = kept([P, 2 * T], U8, "tab_s")
         w2_s = kept([P, 2 * H], U8, "w2_s")
         w3_s = kept([P, N], U8, "w3_s")
-        nc.gpsimd.memset(tab_s[:].bitcast(I32), 0)
+        nc.vector.memset(tab_s[:].bitcast(I32), 0)
         nc.vector.memset(w2_s[:].bitcast(I32), 0)
         nc.vector.memset(w3_s[:].bitcast(I32), 0)
 
         def load_scale_rows(plane, rows):
             for q in range(QUADS):
-                nc.gpsimd.dma_start(
+                nc.sync.dma_start(
                     out=plane[32 * q : 32 * q + 4, :].bitcast(I32).rearrange("r (a c) -> r a c", a=2),
                     in_=rows[:, 4 * q : 4 * q + 4, :].bitcast(I32).rearrange("a r c -> r a c"),
+                )
+
+        def load_packed_scale_rows(plane, rows):
+            for q in range(QUADS):
+                nc.sync.dma_start(
+                    out=plane[32 * q : 32 * q + 8, :].bitcast(I32), in_=rows[:, 4 * q : 4 * q + 4, :].bitcast(I32)
                 )
 
         tab_w = [kept([P, T], I32, f"tab_w{a}") for a in range(2)]
         w2_w = kept([P, 2, H // 2], I32, "w2_w")
         w3_w = kept([P, 2, N], I32, "w3_w")
-        w1_raw = {(a, b): kept([P, PACK, PASS], F32, f"w1_raw{a}{b}") for a in range(2) for b in range(2)}
+        w1_raw = {
+            (a, b): stage.tile([P, PACK, PASS], F32, name=f"w1_raw{a}{b}", tag=f"rows{a}{b}") for b in range(2) for a in range(2)
+        }
         res_sb = {(b, h): kept([P, PACK, HALF], F32, f"res{b}{h}") for b in range(2) for h in range(2)}
         base_sb = kept([P, PACK, PICK], F32, "base_sb")
         temp_sb = kept([P, PACK], F32, "temp_sb")
@@ -73,44 +82,45 @@ def tile_list_monsoon_onset_outlook_kernel(
             rows = res[PASS * b : PASS * (b + 1), HALF * h : HALF * (h + 1)]
             nc.sync.dma_start(out=res_sb[b, h][:], in_=rows.rearrange("(p t) j -> p t j", t=PACK))
 
-        nc.sync.dma_start(offs_sb[:], offs)
-        load_scale_rows(tab_s, tab_scales)
-        for a in range(2):
+        def load_tab_words(a):
             nc.sync.dma_start(out=tab_w[a][:], in_=tab_words[a].rearrange("p t i -> p (t i)").bitcast(I32))
+
+        nc.sync.dma_start(offs_sb[:], offs)
+        load_tab_words(0)
+        load_scale_rows(tab_s, tab_scales)
+        load_w1(0, 0)
         nc.sync.dma_start(out=w2_w[:], in_=w2_words.bitcast(I32).rearrange("a p c -> p a c"))
         load_scale_rows(w2_s, w2_scales)
-        load_w1(0, 0)
         load_w1(1, 0)
-        load_res(0, 0)
+        load_tab_words(1)
         load_w1(0, 1)
+        load_res(0, 0)
         load_w1(1, 1)
         load_res(0, 1)
-        for q in range(QUADS):
-            nc.sync.dma_start(
-                out=w3_s[32 * q : 32 * q + 8, :].bitcast(I32),
-                in_=w3_scales[:, 4 * q : 4 * q + 4, :].bitcast(I32),
-            )
-        load_res(1, 0)
+        load_packed_scale_rows(w3_s, w3_scales)
         nc.sync.dma_start(
             out=w3_w[:], in_=w3_words.rearrange("a p c i -> a p (c i)").bitcast(I32).rearrange("a p c -> p a c")
         )
         load_res(1, 1)
+        load_res(1, 0)
         for vec_sb, vec in ((temp_sb, temp), (sway_sb, sway), (gain_sb, gain)):
             nc.sync.dma_start(out=vec_sb[:], in_=vec.rearrange("(p t) -> p t", t=PACK))
+        nc.sync.dma_start(out=base_sb[:], in_=base.rearrange("(p t) m -> p t m", t=PACK))
         nc.sync.dma_start(pos1_sb[:], pos1)
         nc.sync.dma_start(pos2_sb[:], pos2)
-        nc.sync.dma_start(out=base_sb[:], in_=base.rearrange("(p t) m -> p t m", t=PACK))
 
         v_w, v_s = {}, {}
 
-        def gather_table(h):
-            entries = offs_sb[:, (HALF // 16) * h : (HALF // 16) * (h + 1)]
-            for a in range(2):
+        def gather_words(a):
+            for h in range(2):
+                entries = offs_sb[:, (HALF // 16) * h : (HALF // 16) * (h + 1)]
                 v_w[a, h] = kept([P, HALF], U32, f"v_w{a}{h}")
                 nc.vector.tensor_copy(out=v_w[a, h][:], in_=tab_w[a][:].bitcast(U32).indirect(entries))
+
+        def gather_scales():
             for a in range(2):
-                v_s[a, h] = kept([P, HALF], U8, f"v_s{a}{h}")
-                nc.vector.tensor_copy(out=v_s[a, h][:], in_=tab_s[:, T * a : T * (a + 1)].indirect(entries))
+                v_s[a] = kept([P, S], U8, f"v_s{a}")
+                nc.vector.tensor_copy(out=v_s[a][:], in_=tab_s[:, T * a : T * (a + 1)].indirect(offs_sb[:]))
 
         w2_wd = kept([P, 2, 2, PACK, P], U16, "w2_wd")
         w2_sd = kept([P, 2, 2, PACK, P], U8, "w2_sd")
@@ -128,12 +138,14 @@ def tile_list_monsoon_onset_outlook_kernel(
 
         w1_w, w1_s = {}, {}
 
-        def quantize_w1(a, b):
+        def quantize_w1(a, b, copy):
             grouped = ring.tile([P, PACK, P, PACK], BF16, name="w1_grouped", align_bytes=64)
-            nc.scalar.copy(
-                out=grouped[:].rearrange("p t m i -> p m i t"),
-                in_=w1_raw[a, b][:].rearrange("p i (m t) -> p m i t", t=PACK),
-            )
+            for m0 in range(0, P, P // 2):
+                cols = slice(m0, m0 + P // 2)
+                copy(
+                    out=grouped[:].rearrange("p t m i -> p m i t")[:, cols],
+                    in_=w1_raw[a, b][:].rearrange("p i (m t) -> p m i t", t=PACK)[:, cols],
+                )
             w1_w[a, b] = kept([P, PASS], U32, f"w1_w{a}{b}")
             w1_s[a, b] = kept([P, PASS], U8, f"w1_s{a}{b}")
             nc.vector.quantize_mx(
@@ -143,32 +155,43 @@ def tile_list_monsoon_onset_outlook_kernel(
 
         h_w, h_s = {}, {}
 
-        def first_stage(b, h, adder):
-            best = kept([P, PACK, HALF], F32, f"best{b}{h}")
+        best = {}
+
+        def bank(h, t):
+            return psum.tile([P, HALF], F32, name="acc", tag=f"bank{h}{t}")
+
+        def w2_product(b, h):
+            best[b, h] = stage.tile([P, PACK, HALF], F32, name=f"best{b}{h}", tag=f"rows{(b + h) % 2}{b}")
+            entries = slice(HALF * h, HALF * (h + 1))
             for t in range(PACK):
-                acc = psum.tile([P, HALF], F32, name="acc1")
+                acc = bank(0, t)
                 for a in range(2):
                     nc.tensor.matmul_mx(
                         out=acc[:], lhsT=w2_wd[:, a, b, t, :].bitcast(FP4X4), lhsT_scale=w2_sd[:, a, b, t, :],
-                        rhs=v_w[a, h][:].bitcast(FP8X4), rhs_scale=v_s[a, h][:], start=(a == 0), stop=(a == 1),
+                        rhs=v_w[a, h][:].bitcast(FP8X4), rhs_scale=v_s[a][:, entries], start=(a == 0), stop=(a == 1),
                     )
-                nc.scalar.copy(out=best[:, t, :], in_=acc[:])
+                nc.scalar.copy(out=best[b, h][:, t, :], in_=acc[:])
+
+        def w1_product(b, h):
+            entries = slice(HALF * h, HALF * (h + 1))
             for t in range(PACK):
-                acc = psum.tile([P, HALF], F32, name="acc1")
+                acc = bank(1, t)
                 cols = slice(P * t, P * (t + 1))
                 for a in range(2):
                     nc.tensor.matmul_mx(
                         out=acc[:], lhsT=w1_w[a, b][:, cols].bitcast(FP8X4), lhsT_scale=w1_s[a, b][:, cols],
-                        rhs=v_w[a, h][:].bitcast(FP8X4), rhs_scale=v_s[a, h][:], start=(a == 0), stop=(a == 1),
+                        rhs=v_w[a, h][:].bitcast(FP8X4), rhs_scale=v_s[a][:, entries], start=(a == 0), stop=(a == 1),
                     )
-                nc.vector.tensor_tensor(out=best[:, t, :], in0=acc[:], in1=best[:, t, :], op=ALU.max)
-            grouped = ring.tile([P, HALF * PACK], BF16, name="h_grouped", align_bytes=64)
-            width = HALF // 1
-            for piece in range(1):
+                nc.vector.tensor_tensor(out=best[b, h][:, t, :], in0=acc[:], in1=best[b, h][:, t, :], op=ALU.max)
+
+        def add_and_quantize(b, h, adder, pieces):
+            grouped = kept([P, HALF * PACK], BF16, f"h_grouped{b}{h}")
+            width = HALF // pieces
+            for piece in range(pieces):
                 cols = slice(width * piece, width * (piece + 1))
                 adder.tensor_tensor(
                     out=grouped[:, PACK * cols.start : PACK * cols.stop].rearrange("p (c i t) -> p c t i", i=2, t=PACK),
-                    in0=best[:, :, cols].rearrange("p t (c i) -> p c t i", i=2),
+                    in0=best[b, h][:, :, cols].rearrange("p t (c i) -> p c t i", i=2),
                     in1=res_sb[b, h][:, :, cols].rearrange("p t (c i) -> p c t i", i=2),
                     op=ALU.add,
                 )
@@ -190,15 +213,15 @@ def tile_list_monsoon_onset_outlook_kernel(
         top = [kept([P, PACK], F32, f"top{h}") for h in range(2)]
 
         def second_stage(h, t):
-            acc = psum.tile([P, HALF], F32, name="acc2")
-            for b in range(2):
+            acc = bank(1 - h, t)
+            for b in (1, 0):
                 nc.tensor.matmul_mx(
                     out=acc[:], lhsT=w3_wd[:, b, t, :].bitcast(FP8X4), lhsT_scale=w3_sd[4 * b : P, t, :],
-                    rhs=h_w[b, h][:].bitcast(FP8X4), rhs_scale=h_s[b, h][:], start=(b == 0), stop=(b == 1),
+                    rhs=h_w[b, h][:].bitcast(FP8X4), rhs_scale=h_s[b, h][:], start=(b == 1), stop=(b == 0),
                 )
             nc.vector.tensor_scalar(
                 out=e_sb[t][:, HALF * h : HALF * (h + 1)], in0=acc[:], scalar1=1.0,
-                scalar2=None if h == 0 else top[0][:, t : t + 1],
+                scalar2=None if h == 1 else top[1][:, t : t + 1],
                 op0=ALU.mult, op1=ALU.max, accum_out=top[h][:, t : t + 1],
             )
 
@@ -215,7 +238,7 @@ def tile_list_monsoon_onset_outlook_kernel(
 
         def looks(t):
             col = slice(t, t + 1)
-            nc.scalar.activation(out=shift[:, col], in_=top[1][:, col], func=ACT.Copy, scale=neg_temp[:, col])
+            nc.scalar.activation(out=shift[:, col], in_=top[0][:, col], func=ACT.Copy, scale=neg_temp[:, col])
             onset = ring.tile([P, PICK], F32, name="onset")
             nc.scalar.activation(
                 out=onset[:], in_=e_sb[t][:].indirect(pos1_sb[:]), func=ACT.Exp, bias=shift[:, col], scale=temp_sb[:, col]
@@ -230,23 +253,32 @@ def tile_list_monsoon_onset_outlook_kernel(
             )
             nc.sync.dma_start(out=out_0.rearrange("(p t) m -> p t m", t=PACK)[:, t, :], in_=y[:, t, :])
 
-        gather_table(0)
+        gather_words(0)
+        gather_scales()
+        gather_words(1)
         deal_w2()
-        quantize_w1(0, 0)
-        quantize_w1(1, 0)
-        first_stage(0, 0, nc.vector)
-        gather_table(1)
-        quantize_w1(0, 1)
-        quantize_w1(1, 1)
-        first_stage(0, 1, nc.vector)
-        first_stage(1, 0, nc.vector)
+        quantize_w1(0, 0, nc.scalar.copy)
+        quantize_w1(1, 0, nc.scalar.copy)
+        w2_product(0, 0)
+        w1_product(0, 0)
+        w2_product(0, 1)
+        w1_product(0, 1)
+        add_and_quantize(0, 0, nc.vector, 1)
+        quantize_w1(0, 1, nc.scalar.copy)
+        quantize_w1(1, 1, nc.scalar.copy)
+        add_and_quantize(0, 1, nc.gpsimd, 4)
+        w2_product(1, 0)
+        w1_product(1, 0)
+        w2_product(1, 1)
+        w1_product(1, 1)
         deal_w3()
-        first_stage(1, 1, nc.vector)
-        for t in range(PACK):
-            second_stage(0, t)
-        row_constants()
+        add_and_quantize(1, 1, nc.vector, 1)
         for t in range(PACK):
             second_stage(1, t)
+        add_and_quantize(1, 0, nc.gpsimd, 4)
+        row_constants()
+        for t in range(PACK):
+            second_stage(0, t)
         for t in range(PACK):
             looks(t)
 

@@ -101,8 +101,8 @@ def tile_list_monsoon_onset_outlook_kernel(
         nc.sync.dma_start(
             out=w3_w[:], in_=w3_words.rearrange("a p c i -> a p (c i)").bitcast(I32).rearrange("a p c -> p a c")
         )
-        load_res(1, 1)
         load_res(1, 0)
+        load_res(1, 1)
         for vec_sb, vec in ((temp_sb, temp), (sway_sb, sway), (gain_sb, gain)):
             nc.sync.dma_start(out=vec_sb[:], in_=vec.rearrange("(p t) -> p t", t=PACK))
         nc.sync.dma_start(out=base_sb[:], in_=base.rearrange("(p t) m -> p t m", t=PACK))
@@ -143,8 +143,8 @@ def tile_list_monsoon_onset_outlook_kernel(
             for m0 in range(0, P, P // 2):
                 cols = slice(m0, m0 + P // 2)
                 copy(
-                    out=grouped[:].rearrange("p t m i -> p m i t")[:, cols],
-                    in_=w1_raw[a, b][:].rearrange("p i (m t) -> p m i t", t=PACK)[:, cols],
+                    out=grouped[:].rearrange("p t m i -> p m t i")[:, cols],
+                    in_=w1_raw[a, b][:].rearrange("p i (m t) -> p m t i", t=PACK)[:, cols],
                 )
             w1_w[a, b] = kept([P, PASS], U32, f"w1_w{a}{b}")
             w1_s[a, b] = kept([P, PASS], U8, f"w1_s{a}{b}")
@@ -213,7 +213,7 @@ def tile_list_monsoon_onset_outlook_kernel(
         top = [kept([P, PACK], F32, f"top{h}") for h in range(2)]
 
         def second_stage(h, t):
-            acc = bank(1 - h, t)
+            acc = bank(h, t)
             for b in (1, 0):
                 nc.tensor.matmul_mx(
                     out=acc[:], lhsT=w3_wd[:, b, t, :].bitcast(FP8X4), lhsT_scale=w3_sd[4 * b : P, t, :],
@@ -221,7 +221,7 @@ def tile_list_monsoon_onset_outlook_kernel(
                 )
             nc.vector.tensor_scalar(
                 out=e_sb[t][:, HALF * h : HALF * (h + 1)], in0=acc[:], scalar1=1.0,
-                scalar2=None if h == 1 else top[1][:, t : t + 1],
+                scalar2=None if h == 0 else top[0][:, t : t + 1],
                 op0=ALU.mult, op1=ALU.max, accum_out=top[h][:, t : t + 1],
             )
 
@@ -238,7 +238,7 @@ def tile_list_monsoon_onset_outlook_kernel(
 
         def looks(t):
             col = slice(t, t + 1)
-            nc.scalar.activation(out=shift[:, col], in_=top[0][:, col], func=ACT.Copy, scale=neg_temp[:, col])
+            nc.scalar.activation(out=shift[:, col], in_=top[1][:, col], func=ACT.Copy, scale=neg_temp[:, col])
             onset = ring.tile([P, PICK], F32, name="onset")
             nc.scalar.activation(
                 out=onset[:], in_=e_sb[t][:].indirect(pos1_sb[:]), func=ACT.Exp, bias=shift[:, col], scale=temp_sb[:, col]
@@ -266,19 +266,19 @@ def tile_list_monsoon_onset_outlook_kernel(
         add_and_quantize(0, 0, nc.vector, 1)
         quantize_w1(0, 1, nc.scalar.copy)
         quantize_w1(1, 1, nc.scalar.copy)
-        add_and_quantize(0, 1, nc.gpsimd, 4)
+        add_and_quantize(0, 1, nc.vector, 1)
         w2_product(1, 0)
         w1_product(1, 0)
         w2_product(1, 1)
-        w1_product(1, 1)
         deal_w3()
+        add_and_quantize(1, 0, nc.vector, 1)
+        w1_product(1, 1)
         add_and_quantize(1, 1, nc.vector, 1)
         for t in range(PACK):
-            second_stage(1, t)
-        add_and_quantize(1, 0, nc.gpsimd, 4)
+            second_stage(0, t)
         row_constants()
         for t in range(PACK):
-            second_stage(0, t)
+            second_stage(1, t)
         for t in range(PACK):
             looks(t)
 

from contextlib import ExitStack

import concourse.mybir as mybir

K, H, N, T, S, PICK = 1024, 1024, 512, 2048, 1024, 512
FLOPS = 2 * (2 * K * H * S + H * N * S)

F32 = mybir.dt.float32
BF16 = mybir.dt.bfloat16
I32 = mybir.dt.int32
U32 = mybir.dt.uint32
U16 = mybir.dt.uint16
U8 = mybir.dt.uint8
FP8X4 = mybir.dt.float8_e4m3fn_x4
FP4X4 = mybir.dt.float4_e2m1fn_x4
ALU = mybir.AluOpType
ACT = mybir.ActivationFunctionType

P = 128
PACK = 4
PASS = P * PACK
HALF = 512
QUADS = 4


def tile_list_monsoon_onset_outlook_kernel(
    tc, tab_words, tab_scales, offs, pos1, pos2, w1, w2_words, w2_scales, w3_words, w3_scales,
    res, temp, sway, base, gain, out_0, out_1, out_2,
):
    nc = tc.nc
    with ExitStack() as ctx:
        lists = ctx.enter_context(tc.tile_pool(name="lists", bufs=1))
        keep = ctx.enter_context(tc.tile_pool(name="keep", bufs=1))
        ring = ctx.enter_context(tc.tile_pool(name="ring", bufs=2))
        stage = ctx.enter_context(tc.tile_pool(name="stage", bufs=1))
        psum = ctx.enter_context(tc.psum_pool(name="psum", bufs=1))

        def kept(shape, dtype, name):
            return keep.tile(shape, dtype, name=name, align_bytes=64)

        offs_sb = lists.tile([P, S // 16], U16, name="offs_sb")
        pos1_sb = lists.tile([P, PICK // 16], U16, name="pos1_sb")
        pos2_sb = lists.tile([P, PICK // 16], U16, name="pos2_sb")

        tab_s = kept([P, 2 * T], U8, "tab_s")
        w2_s = kept([P, 2 * H], U8, "w2_s")
        w3_s = kept([P, N], U8, "w3_s")
        nc.vector.memset(tab_s[:].bitcast(I32), 0)
        nc.vector.memset(w2_s[:].bitcast(I32), 0)
        nc.vector.memset(w3_s[:].bitcast(I32), 0)

        def load_scale_rows(plane, rows):
            for q in range(QUADS):
                nc.sync.dma_start(
                    out=plane[32 * q : 32 * q + 4, :].bitcast(I32).rearrange("r (a c) -> r a c", a=2),
                    in_=rows[:, 4 * q : 4 * q + 4, :].bitcast(I32).rearrange("a r c -> r a c"),
                )

        def load_packed_scale_rows(plane, rows):
            for q in range(QUADS):
                nc.sync.dma_start(
                    out=plane[32 * q : 32 * q + 8, :].bitcast(I32), in_=rows[:, 4 * q : 4 * q + 4, :].bitcast(I32)
                )

        tab_w = [kept([P, T], I32, f"tab_w{a}") for a in range(2)]
        w2_w = kept([P, 2, H // 2], I32, "w2_w")
        w3_w = kept([P, 2, N], I32, "w3_w")
        w1_raw = {
            (a, b): stage.tile([P, PACK, PASS], F32, name=f"w1_raw{a}{b}", tag=f"rows{a}{b}") for b in range(2) for a in range(2)
        }
        res_sb = {(b, h): kept([P, PACK, HALF], F32, f"res{b}{h}") for b in range(2) for h in range(2)}
        base_sb = kept([P, PACK, PICK], F32, "base_sb")
        temp_sb = kept([P, PACK], F32, "temp_sb")
        sway_sb = kept([P, PACK], F32, "sway_sb")
        gain_sb = kept([P, PACK], F32, "gain_sb")

        def load_w1(a, b):
            rows = w1[PASS * a : PASS * (a + 1), PASS * b : PASS * (b + 1)]
            nc.sync.dma_start(out=w1_raw[a, b][:], in_=rows.rearrange("(p i) c -> p i c", i=PACK))

        def load_res(b, h):
            rows = res[PASS * b : PASS * (b + 1), HALF * h : HALF * (h + 1)]
            nc.sync.dma_start(out=res_sb[b, h][:], in_=rows.rearrange("(p t) j -> p t j", t=PACK))

        def load_tab_words(a):
            nc.sync.dma_start(out=tab_w[a][:], in_=tab_words[a].rearrange("p t i -> p (t i)").bitcast(I32))

        nc.sync.dma_start(offs_sb[:], offs)
        load_tab_words(0)
        load_scale_rows(tab_s, tab_scales)
        load_w1(0, 0)
        nc.sync.dma_start(out=w2_w[:], in_=w2_words.bitcast(I32).rearrange("a p c -> p a c"))
        load_scale_rows(w2_s, w2_scales)
        load_w1(1, 0)
        load_tab_words(1)
        load_w1(0, 1)
        load_res(0, 0)
        load_w1(1, 1)
        load_res(0, 1)
        load_packed_scale_rows(w3_s, w3_scales)
        nc.sync.dma_start(
            out=w3_w[:], in_=w3_words.rearrange("a p c i -> a p (c i)").bitcast(I32).rearrange("a p c -> p a c")
        )
        load_res(1, 0)
        load_res(1, 1)
        for vec_sb, vec in ((temp_sb, temp), (sway_sb, sway), (gain_sb, gain)):
            nc.sync.dma_start(out=vec_sb[:], in_=vec.rearrange("(p t) -> p t", t=PACK))
        nc.sync.dma_start(out=base_sb[:], in_=base.rearrange("(p t) m -> p t m", t=PACK))
        nc.sync.dma_start(pos1_sb[:], pos1)
        nc.sync.dma_start(pos2_sb[:], pos2)

        v_w, v_s = {}, {}

        def gather_words(a):
            for h in range(2):
                entries = offs_sb[:, (HALF // 16) * h : (HALF // 16) * (h + 1)]
                v_w[a, h] = kept([P, HALF], U32, f"v_w{a}{h}")
                nc.vector.tensor_copy(out=v_w[a, h][:], in_=tab_w[a][:].bitcast(U32).indirect(entries))

        def gather_scales():
            for a in range(2):
                v_s[a] = kept([P, S], U8, f"v_s{a}")
                nc.vector.tensor_copy(out=v_s[a][:], in_=tab_s[:, T * a : T * (a + 1)].indirect(offs_sb[:]))

        w2_wd = kept([P, 2, 2, PACK, P], U16, "w2_wd")
        w2_sd = kept([P, 2, 2, PACK, P], U8, "w2_sd")

        def deal_w2():
            nc.vector.tensor_copy(
                out=w2_sd[:].rearrange("p a b t m -> p (a b) t m"),
                in_=w2_s[:].rearrange("p (ab m t) -> p ab t m", t=PACK, m=P),
            )
            for a in range(2):
                nc.scalar.copy(
                    out=w2_wd[:, a],
                    in_=w2_w[:, a, :].bitcast(U16).rearrange("p (b m t) -> p b t m", t=PACK, m=P),
                )

        w1_w, w1_s = {}, {}

        def quantize_w1(a, b, copy):
            grouped = ring.tile([P, PACK, P, PACK], BF16, name="w1_grouped", align_bytes=64)
            for m0 in range(0, P, P // 2):
                cols = slice(m0, m0 + P // 2)
                copy(
                    out=grouped[:].rearrange("p t m i -> p m t i")[:, cols],
                    in_=w1_raw[a, b][:].rearrange("p i (m t) -> p m t i", t=PACK)[:, cols],
                )
            w1_w[a, b] = kept([P, PASS], U32, f"w1_w{a}{b}")
            w1_s[a, b] = kept([P, PASS], U8, f"w1_s{a}{b}")
            nc.vector.quantize_mx(
                out=w1_w[a, b][:].bitcast(FP8X4), scales=w1_s[a, b][:],
                in_=grouped[:].rearrange("p t m i -> p (t m i)"),
            )

        h_w, h_s = {}, {}

        best = {}

        def bank(h, t):
            return psum.tile([P, HALF], F32, name="acc", tag=f"bank{h}{t}")

        def w2_product(b, h):
            best[b, h] = stage.tile([P, PACK, HALF], F32, name=f"best{b}{h}", tag=f"rows{(b + h) % 2}{b}")
            entries = slice(HALF * h, HALF * (h + 1))
            for t in range(PACK):
                acc = bank(0, t)
                for a in range(2):
                    nc.tensor.matmul_mx(
                        out=acc[:], lhsT=w2_wd[:, a, b, t, :].bitcast(FP4X4), lhsT_scale=w2_sd[:, a, b, t, :],
                        rhs=v_w[a, h][:].bitcast(FP8X4), rhs_scale=v_s[a][:, entries], start=(a == 0), stop=(a == 1),
                    )
                nc.scalar.copy(out=best[b, h][:, t, :], in_=acc[:])

        def w1_product(b, h):
            entries = slice(HALF * h, HALF * (h + 1))
            for t in range(PACK):
                acc = bank(1, t)
                cols = slice(P * t, P * (t + 1))
                for a in range(2):
                    nc.tensor.matmul_mx(
                        out=acc[:], lhsT=w1_w[a, b][:, cols].bitcast(FP8X4), lhsT_scale=w1_s[a, b][:, cols],
                        rhs=v_w[a, h][:].bitcast(FP8X4), rhs_scale=v_s[a][:, entries], start=(a == 0), stop=(a == 1),
                    )
                nc.vector.tensor_tensor(out=best[b, h][:, t, :], in0=acc[:], in1=best[b, h][:, t, :], op=ALU.max)

        def add_and_quantize(b, h, adder, pieces):
            grouped = kept([P, HALF * PACK], BF16, f"h_grouped{b}{h}")
            width = HALF // pieces
            for piece in range(pieces):
                cols = slice(width * piece, width * (piece + 1))
                adder.tensor_tensor(
                    out=grouped[:, PACK * cols.start : PACK * cols.stop].rearrange("p (c i t) -> p c t i", i=2, t=PACK),
                    in0=best[b, h][:, :, cols].rearrange("p t (c i) -> p c t i", i=2),
                    in1=res_sb[b, h][:, :, cols].rearrange("p t (c i) -> p c t i", i=2),
                    op=ALU.add,
                )
            h_w[b, h] = kept([P, HALF], U32, f"h_w{b}{h}")
            h_s[b, h] = kept([P, HALF], U8, f"h_s{b}{h}")
            nc.vector.quantize_mx(out=h_w[b, h][:].bitcast(FP8X4), scales=h_s[b, h][:], in_=grouped[:])

        w3_wd = kept([P, 2, PACK, P], U32, "w3_wd")
        w3_sd = kept([P, PACK, P], U8, "w3_sd")

        def deal_w3():
            nc.vector.tensor_copy(out=w3_sd[:], in_=w3_s[:].rearrange("p (m t) -> p t m", t=PACK))
            nc.scalar.copy(
                out=w3_wd[:].rearrange("p a t m -> p a m t"),
                in_=w3_w[:].bitcast(U32).rearrange("p a (m t) -> p a m t", t=PACK),
            )

        e_sb = [kept([P, S], F32, f"e{t}") for t in range(PACK)]
        top = [kept([P, PACK], F32, f"top{h}") for h in range(2)]

        def second_stage(h, t):
            acc = bank(h, t)
            for b in (1, 0):
                nc.tensor.matmul_mx(
                    out=acc[:], lhsT=w3_wd[:, b, t, :].bitcast(FP8X4), lhsT_scale=w3_sd[4 * b : P, t, :],
                    rhs=h_w[b, h][:].bitcast(FP8X4), rhs_scale=h_s[b, h][:], start=(b == 1), stop=(b == 0),
                )
            nc.vector.tensor_scalar(
                out=e_sb[t][:, HALF * h : HALF * (h + 1)], in0=acc[:], scalar1=1.0,
                scalar2=None if h == 0 else top[0][:, t : t + 1],
                op0=ALU.mult, op1=ALU.max, accum_out=top[h][:, t : t + 1],
            )

        neg_temp = kept([P, PACK], F32, "neg_temp")
        gain_sway = kept([P, PACK], F32, "gain_sway")
        shift = kept([P, PACK], F32, "shift")
        y = kept([P, PACK, PICK], F32, "y")

        def row_constants():
            nc.gpsimd.tensor_scalar(out=neg_temp[:], in0=temp_sb[:], scalar1=-1.0, scalar2=0.0, op0=ALU.mult, op1=ALU.add)
            nc.gpsimd.tensor_tensor(out=gain_sway[:], in0=gain_sb[:], in1=sway_sb[:], op=ALU.mult)
            for t in range(PACK):
                nc.scalar.activation(out=base_sb[:, t, :], in_=base_sb[:, t, :], func=ACT.Copy, scale=gain_sb[:, t : t + 1])

        def looks(t):
            col = slice(t, t + 1)
            nc.scalar.activation(out=shift[:, col], in_=top[1][:, col], func=ACT.Copy, scale=neg_temp[:, col])
            onset = ring.tile([P, PICK], F32, name="onset")
            nc.scalar.activation(
                out=onset[:], in_=e_sb[t][:].indirect(pos1_sb[:]), func=ACT.Exp, bias=shift[:, col], scale=temp_sb[:, col]
            )
            dry = ring.tile([P, PICK], F32, name="dry")
            nc.vector.tensor_copy(out=dry[:], in_=e_sb[t][:].indirect(pos2_sb[:]))
            nc.vector.scalar_tensor_tensor(
                out=dry[:], in0=dry[:], scalar=gain_sb[:, col], in1=base_sb[:, t, :], op0=ALU.mult, op1=ALU.max
            )
            nc.vector.scalar_tensor_tensor(
                out=y[:, t, :], in0=onset[:], scalar=gain_sway[:, col], in1=dry[:], op0=ALU.mult, op1=ALU.add
            )
            nc.sync.dma_start(out=out_0.rearrange("(p t) m -> p t m", t=PACK)[:, t, :], in_=y[:, t, :])

        gather_words(0)
        gather_scales()
        gather_words(1)
        deal_w2()
        quantize_w1(0, 0, nc.scalar.copy)
        quantize_w1(1, 0, nc.scalar.copy)
        w2_product(0, 0)
        w1_product(0, 0)
        w2_product(0, 1)
        w1_product(0, 1)
        add_and_quantize(0, 0, nc.vector, 1)
        quantize_w1(0, 1, nc.scalar.copy)
        quantize_w1(1, 1, nc.scalar.copy)
        add_and_quantize(0, 1, nc.vector, 1)
        w2_product(1, 0)
        w1_product(1, 0)
        w2_product(1, 1)
        deal_w3()
        add_and_quantize(1, 0, nc.vector, 1)
        w1_product(1, 1)
        add_and_quantize(1, 1, nc.vector, 1)
        for t in range(PACK):
            second_stage(0, t)
        row_constants()
        for t in range(PACK):
            second_stage(1, t)
        for t in range(PACK):
            looks(t)

        y_grouped = kept([P, PICK * PACK], BF16, "y_grouped")
        split = 320
        for engine_copy, cols in ((nc.vector.tensor_copy, slice(0, split)), (nc.scalar.copy, slice(split, PICK))):
            engine_copy(
                out=y_grouped[:, PACK * cols.start : PACK * cols.stop].rearrange("p (c i t) -> p c t i", i=4, t=PACK),
                in_=y[:, :, cols].rearrange("p t (c i) -> p c t i", i=4),
            )
        y_w = kept([P, PICK], U32, "y_w")
        y_s = kept([P, PICK], U8, "y_s")
        nc.vector.quantize_mx(out=y_w[:].bitcast(FP8X4), scales=y_s[:], in_=y_grouped[:])
        nc.sync.dma_start(out=out_1[0].rearrange("p m t -> p (m t)").bitcast(I32), in_=y_w[:].bitcast(I32))
        for q in range(QUADS):
            queue = nc.scalar if q % 2 else nc.sync
            queue.dma_start(out=out_2[0, 4 * q : 4 * q + 4, :].bitcast(I32), in_=y_s[32 * q : 32 * q + 4, :].bitcast(I32))
